import numpy as np
import ml_dtypes


def mxq(x, axis, fmt="e4m3"):
    dtype, down = {"e4m3": (ml_dtypes.float8_e4m3fn, 7), "e5m2": (ml_dtypes.float8_e5m2, 14)}[fmt]
    v = np.moveaxis(np.asarray(x, np.float32).astype(ml_dtypes.bfloat16).astype(np.float64), axis, -1)
    blocks = v.reshape(v.shape[:-1] + (-1, 32))
    amax = np.abs(blocks).max(-1, keepdims=True)
    byte = np.maximum(np.where(amax > 0, np.frexp(amax)[1] - 1 + 127, 0) - down, 1)
    scale = np.exp2(byte - 127.0)
    codes = (blocks / scale).astype(np.float32).astype(dtype).astype(np.float64)
    return np.moveaxis((codes * scale).reshape(v.shape), -1, axis)


WIDE = False


def mx_kscale(k):
    if not WIDE:
        return np.ones(k)
    levels = np.array([10, -10, 5, -5, 0])
    if k % 512:
        return np.exp2(np.random.permutation(np.resize(levels, k // 32))).repeat(32)
    a = np.empty((k // 512, 16))
    for p in range(k // 512):
        a[p, :8] = np.random.permutation(np.resize(levels, 8))
        for g in range(8):
            far = levels[np.abs(levels - a[p, g]) >= 10]
            a[p, g + 8] = far[np.random.randint(len(far))]
    return np.exp2(a.ravel()).repeat(32)


def f64(x):
    return np.asarray(x).astype(np.float64)


def striped(idx):
    return np.tile(idx.reshape(-1, 16).T, (8, 1)).astype(np.uint16)


def unstriped(offs):
    return offs[:16].T.reshape(-1).astype(np.int64)


def pack_weight(w):
    k, n = w.shape
    w = f64(np.asarray(w, np.float32).astype(ml_dtypes.bfloat16)).reshape(k // 32, 32, n)
    amax = np.abs(w).max(1)
    byte = np.clip(np.where(amax > 0, np.frexp(amax)[1] - 1 + 127 - 7, 1), 1, 254)
    scaled = (w * np.exp2(127.0 - byte)[:, None, :]).reshape(k, n).astype(np.float32)
    words = np.ascontiguousarray(scaled.reshape(k // 512, 128, 4, n).transpose(0, 1, 3, 2)).astype(ml_dtypes.float8_e4m3fn).view(np.uint8)
    return words, np.ascontiguousarray(byte.astype(np.uint8).reshape(k // 512, 16, n))


def unpack_weight(words, scales):
    g, p, n, _ = words.shape
    vals = np.ascontiguousarray(words).view(ml_dtypes.float8_e4m3fn).astype(np.float64) * np.repeat(np.exp2(scales.astype(np.float64) - 127.0), 8, axis=1)[..., None]
    return vals.transpose(0, 1, 3, 2).reshape(g * 512, n)


K, T, S, D, N, H = 512, 2048, 512, 4, 256, 512


def setup_inputs():
    n = np.random.standard_normal
    s = mx_kscale(K)[:, None]
    u = mx_kscale(H)
    packed_xT = pack_weight(n((K, T)) * s)
    return {
        "x_words": packed_xT[0],
        "x_scales": packed_xT[1],
        "hT": (n((K, H)) / np.sqrt(K) / s).astype(np.float32),
        "sw": (np.random.uniform(0.1, 0.5, (H, S))).astype(np.float32),
        "unit": (np.random.uniform(0.6, 1.4, (H, 1)) * u[:, None]).astype(np.float32),
        "w1": (n((H, N)) / np.sqrt(H) / u[:, None]).astype(np.float32),
        "offs": striped(np.random.permutation(T)[:S]),
        "rec": striped(np.random.permutation(S)),
    }


def reference(x_words, x_scales, hT, sw, unit, w1, offs, rec):
    hTq = mxq(f64(hT), 0, "e4m3")
    xq = unpack_weight(x_words, x_scales)[:, unstriped(offs)]
    y = hTq.T @ xq
    em = np.exp(1.1 * np.tanh(y))
    er = em[:, unstriped(rec)]
    avg = em.mean(axis=1, keepdims=True)
    fwd = (-1.0 * f64(sw) + 1.0) * er + f64(sw) * avg
    post = em * fwd
    ps = post.reshape(len(post), -1, D).sum(axis=2)
    nrm = post / (np.repeat(ps, D, axis=1) + 0.2)
    hid = f64(unit) * (nrm * y - (0.8 * nrm[:, unstriped(rec)]))
    return mxq(f64(w1), 0, "e4m3").T @ mxq(hid, 0, "e4m3")

@@ -1,0 +1,293 @@
+from contextlib import ExitStack
+
+import concourse.mybir as mybir
+from concourse.masks import make_identity
+
+K, T, S, D, N, H = 512, 2048, 512, 4, 256, 512
+FLOPS = 2 * K * H * S + 2 * H * N * S
+
+F32 = mybir.dt.float32
+BF16 = mybir.dt.bfloat16
+I32 = mybir.dt.int32
+U32 = mybir.dt.uint32
+U16 = mybir.dt.uint16
+U8 = mybir.dt.uint8
+FP8X4 = mybir.dt.float8_e4m3fn_x4
+ALU = mybir.AluOpType
+ACT = mybir.ActivationFunctionType
+
+P = 128
+PACK = 4
+G = S // D
+HALF = S // 2
+CHUNKS = ((0, 128), (128, 256), (256, 384), (384, 512))
+
+
+def tile_picked_ypopgn_dos_p_kernel(tc, x_words, x_scales, hT, sw, unit, w1, offs, rec, out):
+    nc = tc.nc
+    with ExitStack() as ctx:
+        sb = ctx.enter_context(tc.tile_pool(name="sb", bufs=1))
+        ps = ctx.enter_context(tc.psum_pool(name="ps", bufs=1))
+
+        offs_t = sb.tile([P, S // 16], U16, name="offs_t")
+        rec_t = sb.tile([P, S // 16], U16, name="rec_t")
+        xw = sb.tile([P, T], U32, name="xw", align_bytes=64)
+        xs = sb.tile([P, T], U8, name="xs", align_bytes=64)
+        h_raw = [sb.tile([P, PACK, H // 2], F32, name="h_raw%d" % a) for a in range(2)]
+        sw_raw = [sb.tile([P, 2, S], F32, name="sw_raw%d" % a) for a in range(2)]
+        w_raw = sb.tile([P, PACK, N], F32, name="w_raw")
+        unit_t = sb.tile([P, PACK], F32, name="unit_t")
+
+        nc.vector.memset(xs[:].bitcast(I32), 0)
+        h_rows = hT.rearrange("(p j) c -> p j c", j=PACK)
+        sw_rows = sw.rearrange("(p t) j -> p t j", t=PACK)
+        nc.sync.dma_start(offs_t[:], offs)
+        nc.sync.dma_start(h_raw[0][:], h_rows[:, :, : H // 2])
+        for q in range(4):
+            nc.sync.dma_start(xs[32 * q : 32 * q + 4, :].bitcast(I32), x_scales[0, 4 * q : 4 * q + 4, :].bitcast(I32))
+        nc.sync.dma_start(h_raw[1][:], h_rows[:, :, H // 2 :])
+        nc.sync.dma_start(xw[:].bitcast(I32), x_words[0].rearrange("p c r -> p (c r)").bitcast(I32))
+        nc.sync.dma_start(sw_raw[0][:], sw_rows[:, 0:2, :])
+        nc.sync.dma_start(sw_raw[1][:], sw_rows[:, 2:4, :])
+        nc.sync.dma_start(rec_t[:], rec)
+        nc.sync.dma_start(unit_t[:], unit.rearrange("(p t) o -> p (t o)", t=PACK))
+        nc.sync.dma_start(w_raw[:], w1.rearrange("(p j) n -> p j n", j=PACK))
+        ident = sb.tile([P, P], F32, name="ident")
+        make_identity(nc, ident[:])
+
+        xs_g = sb.tile([P, S], U8, name="xs_g", align_bytes=64)
+        xw_g = [sb.tile([P, HALF], U32, name="xw_g%d" % a, align_bytes=64) for a in range(2)]
+        h_bf = sb.tile([P, PACK, P, PACK], BF16, name="h_bf", align_bytes=64)
+
+        def round_h(a):
+            nc.vector.tensor_copy(
+                h_bf[:, :, a * 64 : (a + 1) * 64, :].rearrange("p t m j -> p m j t"),
+                h_raw[a][:].rearrange("p j (m t) -> p m j t", t=PACK),
+            )
+
+        round_h(0)
+        nc.vector.tensor_copy(xs_g[:], xs[:].indirect(offs_t[:]))
+        round_h(1)
+        h_codes = sb.tile([P, H], U32, name="h_codes", align_bytes=64)
+        h_scales = sb.tile([P, H], U8, name="h_scales", align_bytes=64)
+        nc.vector.quantize_mx(out=h_codes[:].bitcast(FP8X4), scales=h_scales[:], in_=h_bf[:].rearrange("p t m j -> p (t m j)"))
+        for a in range(2):
+            nc.vector.tensor_copy(xw_g[a][:], xw[:].indirect(offs_t[:, 16 * a : 16 * (a + 1)]))
+        y0 = [ps.tile([P, HALF], F32, name="y0_%d" % a) for a in range(2)]
+        y = [None] + [ps.tile([P, S], F32, name="y%d" % t) for t in range(1, PACK)]
+        for t in range(PACK):
+            for a in range(2):
+                cols = slice(a * HALF, (a + 1) * HALF)
+                nc.tensor.matmul_mx(out=y0[a][:] if t == 0 else y[t][:, cols], lhsT=h_codes[:, t * P : (t + 1) * P].bitcast(FP8X4), lhsT_scale=h_scales[:, t * P : (t + 1) * P],
+                                    rhs=xw_g[a][:].bitcast(FP8X4), rhs_scale=xs_g[:, cols], start=True, stop=True)
+
+        def rows(name, width, count=PACK):
+            return [sb.tile([P, width], F32, name="%s%d" % (name, t), align_bytes=64) for t in range(count)]
+
+        stay, em, er, mix, post, nrm = [rows(name, S) for name in ("stay", "em", "er", "mix", "post", "nrm")]
+        total, avg = rows("total", 1), rows("avg", 1)
+        half, den, inv = rows("half", 2 * G), rows("den", G), rows("inv", G)
+        both, inv_both = rows("both", G), rows("inv_both", G)
+        own = sb.tile([P, PACK, S], F32, name="own")
+        prev = [sb.tile([P, PACK, hi - lo], F32, name="prev%d" % c) for c, (lo, hi) in enumerate(CHUNKS)]
+        gain = sb.tile([P, PACK], F32, name="gain")
+        w_codes = sb.tile([P, N], U32, name="w_codes", align_bytes=64)
+        w_scales = sb.tile([P, N], U8, name="w_scales", align_bytes=64)
+        scale = [inv[t][:] for t in range(PACK)]
+
+        def emission(t):
+            th = sb.tile([P, S], F32, name="th")
+            if t == 0:
+                for a in range(2):
+                    nc.scalar.activation(th[:, a * HALF : (a + 1) * HALF], y0[a][:], ACT.Tanh)
+            else:
+                nc.scalar.activation(th[:], y[t][:], ACT.Tanh)
+            nc.scalar.activation(em[t][:], th[:], ACT.Exp, scale=1.1, accum_out=total[t][:])
+            nc.scalar.activation(avg[t][:], total[t][:], ACT.Copy, scale=1.0 / S)
+
+        def stay_v(t):
+            nc.vector.tensor_scalar(stay[t][:], sw_raw[t // 2][:, t % 2, :], -1.0, 1.0, ALU.mult, ALU.add)
+
+        def stay_s(t):
+            nc.scalar.activation(stay[t][:], sw_raw[t // 2][:, t % 2, :], ACT.Copy, scale=-1.0, bias=1.0)
+
+        def stay_g(t):
+            nc.gpsimd.tensor_scalar(stay[t][:], sw_raw[t // 2][:, t % 2, :], -1.0, 1.0, ALU.mult, ALU.add)
+
+        def fetch_er(t, on_vector):
+            cuts = sorted(set([0, on_vector, S] + ([HALF] if on_vector in (0, S) else [])))
+            for lo, hi in zip(cuts, cuts[1:]):
+                picked = em[t][:].indirect(rec_t[:, lo // 16 : hi // 16])
+                if hi <= on_vector:
+                    nc.vector.tensor_copy(er[t][:, lo:hi], picked)
+                else:
+                    nc.scalar.activation(er[t][:, lo:hi], picked, ACT.Copy)
+
+        def mixed(t):
+            nc.vector.scalar_tensor_tensor(mix[t][:], er[t][:], avg[t][:], stay[t][:], ALU.subtract, ALU.mult)
+
+        def posterior(t):
+            nc.vector.scalar_tensor_tensor(post[t][:], mix[t][:], avg[t][:], em[t][:], ALU.add, ALU.mult)
+
+        def group_sum(t):
+            groups = post[t][:].rearrange("p (v d) -> p v d", d=D)
+            pairs = half[t][:].rearrange("p (v d) -> p v d", d=2)
+            nc.vector.tensor_tensor(pairs, groups[:, :, 0:2], groups[:, :, 2:4], ALU.add)
+            nc.vector.scalar_tensor_tensor(den[t][:], pairs[:, :, 0], 0.2, pairs[:, :, 1], ALU.add, ALU.add)
+
+        def mixed_part(t, a):
+            cols = slice(a * HALF, (a + 1) * HALF)
+            nc.vector.scalar_tensor_tensor(mix[t][:, cols], er[t][:, cols], avg[t][:], stay[t][:, cols], ALU.subtract, ALU.mult)
+
+        def posterior_part(t, a):
+            cols = slice(a * HALF, (a + 1) * HALF)
+            nc.vector.scalar_tensor_tensor(post[t][:, cols], mix[t][:, cols], avg[t][:], em[t][:, cols], ALU.add, ALU.mult)
+
+        def invert_halves(t):
+            two = den[t][:].rearrange("p (e v) -> p e v", e=2)
+            nc.vector.tensor_tensor(both[t][:, : G // 2], two[:, 0, :], two[:, 1, :], ALU.mult)
+            nc.vector.reciprocal(inv_both[t][:, : G // 2], both[t][:, : G // 2])
+            nc.vector.tensor_tensor(inv[t][:].rearrange("p (e v) -> p e v", e=2), two[:, ::-1, :],
+                                    inv_both[t][:, : G // 2].unsqueeze(1).to_broadcast([P, 2, G // 2]), ALU.mult)
+
+        def turn_back(t):
+            back = ps.tile([P, G], F32, name="back")
+            nc.tensor.transpose(back[:], inv[t][:], ident[:])
+            scale[t] = back[:]
+
+        def invert_one(t):
+            nc.vector.reciprocal(inv[t][:], den[t][:])
+
+        def invert_pair(a, b):
+            nc.vector.tensor_tensor(both[a][:], den[a][:], den[b][:], ALU.mult)
+            nc.vector.reciprocal(inv_both[a][:], both[a][:])
+            nc.vector.tensor_tensor(inv[a][:], inv_both[a][:], den[b][:], ALU.mult)
+            nc.vector.tensor_tensor(inv[b][:], inv_both[a][:], den[a][:], ALU.mult)
+
+        def group_sum_turned(t, first=None):
+            acc = ps.tile([P, P], F32, name="sum_t%d" % (t % 2))
+            groups = post[t][:].rearrange("p (v d) -> p v d", d=D)
+            for d in range(D):
+                nc.tensor.matmul(out=acc[:], lhsT=groups[:, :, d], rhs=ident[:], is_transpose=True, start=d == 0, stop=d == D - 1)
+            if (t % 2 == 0 if first is None else first):
+                nc.scalar.activation(den[t][:], acc[:], ACT.Copy, bias=0.2)
+            return acc
+
+        def invert_pair_turned(a, b, sum_b):
+            nc.vector.scalar_tensor_tensor(both[a][:], sum_b[:], 0.2, den[a][:], ALU.add, ALU.mult)
+            nc.vector.reciprocal(inv_both[a][:], both[a][:])
+            nc.vector.scalar_tensor_tensor(inv[a][:], sum_b[:], 0.2, inv_both[a][:], ALU.add, ALU.mult)
+            nc.vector.tensor_tensor(inv[b][:], inv_both[a][:], den[a][:], ALU.mult)
+            back = ps.tile([P, 2, G], F32, name="back")
+            nc.tensor.transpose(back[:, 0, :], inv[a][:], ident[:])
+            nc.tensor.transpose(back[:, 1, :], inv[b][:], ident[:])
+            scale[a] = back[:, 0, :]
+            scale[b] = back[:, 1, :]
+
+        def round_w(copy, tag):
+            w_bf = sb.tile([P, N, PACK], BF16, name="w_bf", tag=tag, align_bytes=64)
+            copy(w_bf[:].rearrange("p (c i) j -> p c j i", i=4), w_raw[:].rearrange("p j (c i) -> p c j i", i=4))
+            nc.vector.quantize_mx(out=w_codes[:].bitcast(FP8X4), scales=w_scales[:], in_=w_bf[:].rearrange("p n j -> p (n j)"))
+
+        def normalise(t):
+            nc.vector.scalar_tensor_tensor(
+                nrm[t][:].rearrange("p (v d) -> p v d", d=D),
+                post[t][:].rearrange("p (v d) -> p v d", d=D),
+                gain[:, t : t + 1],
+                scale[t].unsqueeze(2).to_broadcast([P, G, D]),
+                ALU.mult, ALU.mult)
+
+        def own_term(t):
+            if t == 0:
+                for a in range(2):
+                    cols = slice(a * HALF, (a + 1) * HALF)
+                    nc.vector.scalar_tensor_tensor(own[:, 0, cols], y0[a][:], -1.25, nrm[0][:, cols], ALU.mult, ALU.mult)
+            else:
+                nc.vector.scalar_tensor_tensor(own[:, t, :], y[t][:], -1.25, nrm[t][:], ALU.mult, ALU.mult)
+
+        def fetch_prev(t, c):
+            lo, hi = CHUNKS[c]
+            nc.scalar.activation(prev[c][:, t, :], nrm[t][:].indirect(rec_t[:, lo // 16 : hi // 16]), ACT.Copy)
+
+        BANKS = ["y0_0", "y0_1", "y1", "y2", "y3"]
+        stay_v(0)
+        stay_v(1)
+        stay_v(2)
+        stay_v(3)
+        emission(0)
+        fetch_er(0, 512)
+        emission(1)
+        fetch_er(1, 0)
+        nc.scalar.activation(gain[:], unit_t[:], ACT.Copy, scale=-0.8)
+        mixed_part(0, 0)
+        mixed_part(0, 1)
+        posterior_part(0, 0)
+        posterior_part(0, 1)
+        group_sum(0)
+        invert_halves(0)
+        mixed(1)
+        posterior(1)
+        group_sum_turned(1, True)
+        normalise(0)
+        emission(2)
+        fetch_er(2, 0)
+        emission(3)
+        fetch_er(3, 0)
+        own_term(0)
+        invert_halves(1)
+        turn_back(1)
+        mixed(2)
+        posterior(2)
+        group_sum_turned(2, True)
+
+        normalise(1)
+        mixed(3)
+        posterior(3)
+        group_sum(3)
+        invert_halves(2)
+        turn_back(2)
+        invert_halves(3)
+
+        for c in range(len(CHUNKS)):
+            fetch_prev(0, c)
+        round_w(nc.scalar.copy, "er3")
+        normalise(2)
+        normalise(3)
+        for c in range(len(CHUNKS)):
+            fetch_prev(1, c)
+        for c in range(len(CHUNKS)):
+            fetch_prev(2, c)
+        for c in range(len(CHUNKS)):
+            fetch_prev(3, c)
+        own_term(1)
+        own_term(2)
+        own_term(3)
+
+        out_rows = out.rearrange("(h p) j -> p h j", p=P)
+        for c, (lo, hi) in enumerate(CHUNKS):
+            cols = slice(lo, hi)
+            width = hi - lo
+            hid = sb.tile([P, width, PACK], BF16, name="hid%d" % c, align_bytes=64)
+            nc.vector.tensor_tensor(
+                hid[:].rearrange("p (c i) t -> p c t i", i=4),
+                own[:, :, cols].rearrange("p t (c i) -> p c t i", i=4),
+                prev[c][:].rearrange("p t (c i) -> p c t i", i=4),
+                ALU.add)
+            hid_codes = sb.tile([P, width], U32, name="hid_codes%d" % c, align_bytes=64)
+            hid_scales = sb.tile([P, width], U8, name="hid_scales%d" % c, align_bytes=64)
+            nc.vector.quantize_mx(out=hid_codes[:].bitcast(FP8X4), scales=hid_scales[:], in_=hid[:].rearrange("p j t -> p (j t)"))
+            last = c == len(CHUNKS) - 1
+            acc = [ps.tile([P, width], F32, name="acc_last%d" % h, tag=BANKS[c + h])[:] for h in range(2)] if last else None
+            if not last:
+                bank = ps.tile([P, 2, width], F32, name="acc%d" % c, tag=BANKS[c])
+                acc = [bank[:, h, :] for h in range(2)]
+            for h in range(N // P):
+                nc.tensor.matmul_mx(out=acc[h], lhsT=w_codes[:, h * P : (h + 1) * P].bitcast(FP8X4), lhsT_scale=w_scales[:, h * P : (h + 1) * P],
+                                    rhs=hid_codes[:].bitcast(FP8X4), rhs_scale=hid_scales[:], start=True, stop=True)
+            res = sb.tile([P, 2, width], F32, name="res%d" % c)
+            if last:
+                nc.scalar.copy(res[:, 0, :], acc[0])
+                nc.vector.tensor_copy(res[:, 1, :], acc[1])
+            else:
+                nc.scalar.copy(res[:], bank[:])
+            nc.sync.dma_start(out_rows[:, :, cols], res[:])

@@ -3,7 +3,7 @@ from contextlib import ExitStack
 import concourse.mybir as mybir
 from concourse.masks import make_identity
 
-K, T, S, D, N, H = 512, 2048, 512, 4, 256, 512
+K, S, T, D, N, H = 512, 512, 2048, 4, 256, 512
 FLOPS = 2 * K * H * S + 2 * H * N * S
 
 F32 = mybir.dt.float32
@@ -18,9 +18,13 @@ ACT = mybir.ActivationFunctionType
 
 P = 128
 PACK = 4
-G = S // D
+LANES = 16
+GROUPS = S // D
 HALF = S // 2
-CHUNKS = ((0, 128), (128, 256), (256, 384), (384, 512))
+WHOLE = slice(0, S)
+HALVES = (slice(0, HALF), slice(HALF, S))
+LAST = PACK - 1
+STRETCHES = ((0, 128), (128, 256), (256, 320), (320, 384), (384, 448), (448, 512))
 
 
 def tile_picked_ypopgn_dos_p_kernel(tc, x_words, x_scales, hT, sw, unit, w1, offs, rec, out):
@@ -29,265 +33,230 @@ def tile_picked_ypopgn_dos_p_kernel(tc, x_words, x_scales, hT, sw, unit, w1, off
         sb = ctx.enter_context(tc.tile_pool(name="sb", bufs=1))
         ps = ctx.enter_context(tc.psum_pool(name="ps", bufs=1))
 
-        offs_t = sb.tile([P, S // 16], U16, name="offs_t")
-        rec_t = sb.tile([P, S // 16], U16, name="rec_t")
-        xw = sb.tile([P, T], U32, name="xw", align_bytes=64)
-        xs = sb.tile([P, T], U8, name="xs", align_bytes=64)
-        h_raw = [sb.tile([P, PACK, H // 2], F32, name="h_raw%d" % a) for a in range(2)]
+        def floats(name, width, tag=None):
+            return sb.tile([P, width], F32, name=name, tag=tag or name, align_bytes=64)
+
+        def row_tiles(name, width):
+            return [floats("%s%d" % (name, t), width) for t in range(PACK)]
+
+        def picked(window, places, cols):
+            return window[:].indirect(places[:, cols.start // LANES : cols.stop // LANES])
+
+        offs_t = sb.tile([P, S // LANES], U16, name="offs_t")
+        rec_t = sb.tile([P, S // LANES], U16, name="rec_t")
+        words = sb.tile([P, T], U32, name="words", align_bytes=64)
+        scales = sb.tile([P, T], U8, name="scales", align_bytes=64)
+        h_raw = sb.tile([P, PACK, H], F32, name="h_raw")
         sw_raw = [sb.tile([P, 2, S], F32, name="sw_raw%d" % a) for a in range(2)]
         w_raw = sb.tile([P, PACK, N], F32, name="w_raw")
         unit_t = sb.tile([P, PACK], F32, name="unit_t")
 
-        nc.vector.memset(xs[:].bitcast(I32), 0)
-        h_rows = hT.rearrange("(p j) c -> p j c", j=PACK)
+        nc.vector.memset(scales[:].bitcast(I32), 0)
         sw_rows = sw.rearrange("(p t) j -> p t j", t=PACK)
+        nc.sync.dma_start(h_raw[:], hT.rearrange("(p r) c -> p r c", r=PACK))
         nc.sync.dma_start(offs_t[:], offs)
-        nc.sync.dma_start(h_raw[0][:], h_rows[:, :, : H // 2])
-        for q in range(4):
-            nc.sync.dma_start(xs[32 * q : 32 * q + 4, :].bitcast(I32), x_scales[0, 4 * q : 4 * q + 4, :].bitcast(I32))
-        nc.sync.dma_start(h_raw[1][:], h_rows[:, :, H // 2 :])
-        nc.sync.dma_start(xw[:].bitcast(I32), x_words[0].rearrange("p c r -> p (c r)").bitcast(I32))
+        for a in range(4):
+            nc.sync.dma_start(scales[a:P:32, :].bitcast(I32), x_scales[0, a:16:4, :].bitcast(I32))
+        nc.sync.dma_start(words[:].bitcast(I32), x_words[0].rearrange("p c r -> p (c r)").bitcast(I32))
+        nc.sync.dma_start(w_raw[:], w1.rearrange("(p r) n -> p r n", r=PACK))
         nc.sync.dma_start(sw_raw[0][:], sw_rows[:, 0:2, :])
-        nc.sync.dma_start(sw_raw[1][:], sw_rows[:, 2:4, :])
         nc.sync.dma_start(rec_t[:], rec)
+        nc.sync.dma_start(sw_raw[1][:], sw_rows[:, 2:4, :])
         nc.sync.dma_start(unit_t[:], unit.rearrange("(p t) o -> p (t o)", t=PACK))
-        nc.sync.dma_start(w_raw[:], w1.rearrange("(p j) n -> p j n", j=PACK))
         ident = sb.tile([P, P], F32, name="ident")
         make_identity(nc, ident[:])
 
-        xs_g = sb.tile([P, S], U8, name="xs_g", align_bytes=64)
-        xw_g = [sb.tile([P, HALF], U32, name="xw_g%d" % a, align_bytes=64) for a in range(2)]
-        h_bf = sb.tile([P, PACK, P, PACK], BF16, name="h_bf", align_bytes=64)
-
-        def round_h(a):
-            nc.vector.tensor_copy(
-                h_bf[:, :, a * 64 : (a + 1) * 64, :].rearrange("p t m j -> p m j t"),
-                h_raw[a][:].rearrange("p j (m t) -> p m j t", t=PACK),
-            )
-
-        round_h(0)
-        nc.vector.tensor_copy(xs_g[:], xs[:].indirect(offs_t[:]))
-        round_h(1)
-        h_codes = sb.tile([P, H], U32, name="h_codes", align_bytes=64)
+        scales_g = sb.tile([P, S], U8, name="scales_g", align_bytes=64)
+        words_g = [sb.tile([P, HALF], U32, name="words_g%d" % a, align_bytes=64) for a in range(2)]
+        h_bf = [sb.tile([P, 2, P, PACK], BF16, name="h_bf%d" % a, align_bytes=64) for a in range(2)]
+        h_cols = h_raw[:].rearrange("p r (m t) -> p m r t", t=PACK)
+        nc.vector.tensor_copy(h_bf[0][:].rearrange("p u m r -> p m r u"), h_cols[:, :, :, 0:2])
+        nc.scalar.copy(h_bf[1][:].rearrange("p u m r -> p m r u"), h_cols[:, :, :, 2:4])
+        nc.vector.tensor_copy(scales_g[:], picked(scales, offs_t, WHOLE))
+        h_codes = sb.tile([P, H], U32, name="h_codes", tag="scales", align_bytes=64)
         h_scales = sb.tile([P, H], U8, name="h_scales", align_bytes=64)
-        nc.vector.quantize_mx(out=h_codes[:].bitcast(FP8X4), scales=h_scales[:], in_=h_bf[:].rearrange("p t m j -> p (t m j)"))
         for a in range(2):
-            nc.vector.tensor_copy(xw_g[a][:], xw[:].indirect(offs_t[:, 16 * a : 16 * (a + 1)]))
-        y0 = [ps.tile([P, HALF], F32, name="y0_%d" % a) for a in range(2)]
-        y = [None] + [ps.tile([P, S], F32, name="y%d" % t) for t in range(1, PACK)]
+            pair = slice(a * 2 * P, (a + 1) * 2 * P)
+            nc.vector.quantize_mx(out=h_codes[:, pair].bitcast(FP8X4), scales=h_scales[:, pair],
+                                  in_=h_bf[a][:].rearrange("p u m r -> p (u m r)"))
+        for a in range(2):
+            nc.vector.tensor_copy(words_g[a][:], picked(words, offs_t, HALVES[a]))
+        y = [[ps.tile([P, HALF], F32, name="y0_%d" % a)[:] for a in range(2)]]
+        for t in range(1, PACK):
+            bank = ps.tile([P, S], F32, name="y%d" % t)
+            y.append([bank[:, cols] for cols in HALVES] + [bank[:]])
         for t in range(PACK):
+            profiles = slice(t * P, (t + 1) * P)
             for a in range(2):
-                cols = slice(a * HALF, (a + 1) * HALF)
-                nc.tensor.matmul_mx(out=y0[a][:] if t == 0 else y[t][:, cols], lhsT=h_codes[:, t * P : (t + 1) * P].bitcast(FP8X4), lhsT_scale=h_scales[:, t * P : (t + 1) * P],
-                                    rhs=xw_g[a][:].bitcast(FP8X4), rhs_scale=xs_g[:, cols], start=True, stop=True)
+                nc.tensor.matmul_mx(out=y[t][a], lhsT=h_codes[:, profiles].bitcast(FP8X4), lhsT_scale=h_scales[:, profiles],
+                                    rhs=words_g[a][:].bitcast(FP8X4), rhs_scale=scales_g[:, HALVES[a]], start=True, stop=True)
 
-        def rows(name, width, count=PACK):
-            return [sb.tile([P, width], F32, name="%s%d" % (name, t), align_bytes=64) for t in range(count)]
-
-        stay, em, er, mix, post, nrm = [rows(name, S) for name in ("stay", "em", "er", "mix", "post", "nrm")]
-        total, avg = rows("total", 1), rows("avg", 1)
-        half, den, inv = rows("half", 2 * G), rows("den", G), rows("inv", G)
-        both, inv_both = rows("both", G), rows("inv_both", G)
-        own = sb.tile([P, PACK, S], F32, name="own")
-        prev = [sb.tile([P, PACK, hi - lo], F32, name="prev%d" % c) for c, (lo, hi) in enumerate(CHUNKS)]
+        stay, er, nrm = row_tiles("stay", S), row_tiles("er", S), row_tiles("nrm", S)
+        em_win = row_tiles("em", S + 1)
+        avg = row_tiles("avg", 1)
+        mix = [floats("mix%d" % t, S, tag="mix") for t in range(PACK)]
+        own = sb.tile([P, PACK, S], F32, name="own", tag="mix", align_bytes=64)
+        prev = [sb.tile([P, PACK, HALF], F32, name="prev%d" % a) for a in range(2)]
+        post = [floats("post%d" % t, S)[:] for t in range(LAST)] + [prev[1][:, 2:4, :].rearrange("p t j -> p (t j)")]
         gain = sb.tile([P, PACK], F32, name="gain")
+        w_bf = sb.tile([P, N, PACK], BF16, name="w_bf", align_bytes=64)
         w_codes = sb.tile([P, N], U32, name="w_codes", align_bytes=64)
         w_scales = sb.tile([P, N], U8, name="w_scales", align_bytes=64)
-        scale = [inv[t][:] for t in range(PACK)]
+        floor = sb.tile([P, P], F32, name="floor")
+        nc.gpsimd.memset(floor[:], 1.0)
+        nc.gpsimd.tensor_scalar(floor[:], floor[:], 0.2, 0.0, ALU.mult, ALU.add)
 
         def emission(t):
-            th = sb.tile([P, S], F32, name="th")
-            if t == 0:
-                for a in range(2):
-                    nc.scalar.activation(th[:, a * HALF : (a + 1) * HALF], y0[a][:], ACT.Tanh)
-            else:
-                nc.scalar.activation(th[:], y[t][:], ACT.Tanh)
-            nc.scalar.activation(em[t][:], th[:], ACT.Exp, scale=1.1, accum_out=total[t][:])
-            nc.scalar.activation(avg[t][:], total[t][:], ACT.Copy, scale=1.0 / S)
+            bent = floats("bent%d" % t, S)
+            for a in range(2):
+                nc.scalar.activation(bent[:, HALVES[a]], y[t][a], ACT.Tanh)
+            nc.scalar.activation(em_win[t][:, :S], bent[:], ACT.Exp, scale=1.1, accum_out=em_win[t][:, S:])
+            nc.scalar.activation(avg[t][:], em_win[t][:, S:], ACT.Copy, scale=1.0 / S)
 
-        def stay_v(t):
+        def stay_on_vector(t):
             nc.vector.tensor_scalar(stay[t][:], sw_raw[t // 2][:, t % 2, :], -1.0, 1.0, ALU.mult, ALU.add)
 
-        def stay_s(t):
-            nc.scalar.activation(stay[t][:], sw_raw[t // 2][:, t % 2, :], ACT.Copy, scale=-1.0, bias=1.0)
+        def fetch_er(t):
+            nc.scalar.activation(er[t][:], picked(em_win[t], rec_t, WHOLE), ACT.Copy)
 
-        def stay_g(t):
-            nc.gpsimd.tensor_scalar(stay[t][:], sw_raw[t // 2][:, t % 2, :], -1.0, 1.0, ALU.mult, ALU.add)
-
-        def fetch_er(t, on_vector):
-            cuts = sorted(set([0, on_vector, S] + ([HALF] if on_vector in (0, S) else [])))
-            for lo, hi in zip(cuts, cuts[1:]):
-                picked = em[t][:].indirect(rec_t[:, lo // 16 : hi // 16])
-                if hi <= on_vector:
-                    nc.vector.tensor_copy(er[t][:, lo:hi], picked)
-                else:
-                    nc.scalar.activation(er[t][:, lo:hi], picked, ACT.Copy)
-
-        def mixed(t):
-            nc.vector.scalar_tensor_tensor(mix[t][:], er[t][:], avg[t][:], stay[t][:], ALU.subtract, ALU.mult)
-
-        def posterior(t):
-            nc.vector.scalar_tensor_tensor(post[t][:], mix[t][:], avg[t][:], em[t][:], ALU.add, ALU.mult)
-
-        def group_sum(t):
-            groups = post[t][:].rearrange("p (v d) -> p v d", d=D)
-            pairs = half[t][:].rearrange("p (v d) -> p v d", d=2)
-            nc.vector.tensor_tensor(pairs, groups[:, :, 0:2], groups[:, :, 2:4], ALU.add)
-            nc.vector.scalar_tensor_tensor(den[t][:], pairs[:, :, 0], 0.2, pairs[:, :, 1], ALU.add, ALU.add)
-
-        def mixed_part(t, a):
-            cols = slice(a * HALF, (a + 1) * HALF)
+        def mixed(t, cols):
             nc.vector.scalar_tensor_tensor(mix[t][:, cols], er[t][:, cols], avg[t][:], stay[t][:, cols], ALU.subtract, ALU.mult)
 
-        def posterior_part(t, a):
-            cols = slice(a * HALF, (a + 1) * HALF)
-            nc.vector.scalar_tensor_tensor(post[t][:, cols], mix[t][:, cols], avg[t][:], em[t][:, cols], ALU.add, ALU.mult)
+        def posterior(t, cols):
+            nc.vector.scalar_tensor_tensor(post[t][:, cols], mix[t][:, cols], avg[t][:], em_win[t][:, cols], ALU.add, ALU.mult)
 
-        def invert_halves(t):
-            two = den[t][:].rearrange("p (e v) -> p e v", e=2)
-            nc.vector.tensor_tensor(both[t][:, : G // 2], two[:, 0, :], two[:, 1, :], ALU.mult)
-            nc.vector.reciprocal(inv_both[t][:, : G // 2], both[t][:, : G // 2])
-            nc.vector.tensor_tensor(inv[t][:].rearrange("p (e v) -> p e v", e=2), two[:, ::-1, :],
-                                    inv_both[t][:, : G // 2].unsqueeze(1).to_broadcast([P, 2, G // 2]), ALU.mult)
+        def posterior_by_halves(t):
+            for step in (mixed, posterior):
+                for cols in HALVES:
+                    step(t, cols)
 
-        def turn_back(t):
-            back = ps.tile([P, G], F32, name="back")
-            nc.tensor.transpose(back[:], inv[t][:], ident[:])
-            scale[t] = back[:]
+        def group_sums(t):
+            turned = ps.tile([P, P], F32, name="turned%d" % t, tag="sum%d" % t)
+            members = post[t].rearrange("p (v d) -> p v d", d=D)
+            terms = [floor[:]] + [members[:, :, d] for d in range(D)]
+            for n, term in enumerate(terms):
+                nc.tensor.matmul(out=turned[:], lhsT=term, rhs=ident[:], is_transpose=True, start=n == 0, stop=n == D)
+            return turned
 
-        def invert_one(t):
-            nc.vector.reciprocal(inv[t][:], den[t][:])
+        def invert(t, turned, tag):
+            inverse = floats("inverse%d" % t, GROUPS, tag=tag)
+            nc.vector.reciprocal(inverse[:], turned[:])
+            return inverse
 
-        def invert_pair(a, b):
-            nc.vector.tensor_tensor(both[a][:], den[a][:], den[b][:], ALU.mult)
-            nc.vector.reciprocal(inv_both[a][:], both[a][:])
-            nc.vector.tensor_tensor(inv[a][:], inv_both[a][:], den[b][:], ALU.mult)
-            nc.vector.tensor_tensor(inv[b][:], inv_both[a][:], den[a][:], ALU.mult)
+        def turn_back(t, inverse):
+            back = ps.tile([P, GROUPS], F32, name="back%d" % t, tag="sum%d" % t)
+            nc.tensor.transpose(back[:], inverse[:], ident[:])
+            return back
 
-        def group_sum_turned(t, first=None):
-            acc = ps.tile([P, P], F32, name="sum_t%d" % (t % 2))
-            groups = post[t][:].rearrange("p (v d) -> p v d", d=D)
-            for d in range(D):
-                nc.tensor.matmul(out=acc[:], lhsT=groups[:, :, d], rhs=ident[:], is_transpose=True, start=d == 0, stop=d == D - 1)
-            if (t % 2 == 0 if first is None else first):
-                nc.scalar.activation(den[t][:], acc[:], ACT.Copy, bias=0.2)
-            return acc
-
-        def invert_pair_turned(a, b, sum_b):
-            nc.vector.scalar_tensor_tensor(both[a][:], sum_b[:], 0.2, den[a][:], ALU.add, ALU.mult)
-            nc.vector.reciprocal(inv_both[a][:], both[a][:])
-            nc.vector.scalar_tensor_tensor(inv[a][:], sum_b[:], 0.2, inv_both[a][:], ALU.add, ALU.mult)
-            nc.vector.tensor_tensor(inv[b][:], inv_both[a][:], den[a][:], ALU.mult)
-            back = ps.tile([P, 2, G], F32, name="back")
-            nc.tensor.transpose(back[:, 0, :], inv[a][:], ident[:])
-            nc.tensor.transpose(back[:, 1, :], inv[b][:], ident[:])
-            scale[a] = back[:, 0, :]
-            scale[b] = back[:, 1, :]
-
-        def round_w(copy, tag):
-            w_bf = sb.tile([P, N, PACK], BF16, name="w_bf", tag=tag, align_bytes=64)
-            copy(w_bf[:].rearrange("p (c i) j -> p c j i", i=4), w_raw[:].rearrange("p j (c i) -> p c j i", i=4))
-            nc.vector.quantize_mx(out=w_codes[:].bitcast(FP8X4), scales=w_scales[:], in_=w_bf[:].rearrange("p n j -> p (n j)"))
-
-        def normalise(t):
+        def normalise(t, inverse):
             nc.vector.scalar_tensor_tensor(
-                nrm[t][:].rearrange("p (v d) -> p v d", d=D),
-                post[t][:].rearrange("p (v d) -> p v d", d=D),
-                gain[:, t : t + 1],
-                scale[t].unsqueeze(2).to_broadcast([P, G, D]),
-                ALU.mult, ALU.mult)
+                nrm[t][:].rearrange("p (v d) -> p v d", d=D), post[t].rearrange("p (v d) -> p v d", d=D), gain[:, t : t + 1],
+                inverse[:].unsqueeze(2).to_broadcast([P, GROUPS, D]), ALU.mult, ALU.mult)
 
-        def own_term(t):
-            if t == 0:
-                for a in range(2):
-                    cols = slice(a * HALF, (a + 1) * HALF)
-                    nc.vector.scalar_tensor_tensor(own[:, 0, cols], y0[a][:], -1.25, nrm[0][:, cols], ALU.mult, ALU.mult)
-            else:
-                nc.vector.scalar_tensor_tensor(own[:, t, :], y[t][:], -1.25, nrm[t][:], ALU.mult, ALU.mult)
+        def fetch_prev(t, lo, hi):
+            first = lo % HALF
+            nc.scalar.activation(prev[lo // HALF][:, t, first : first + hi - lo], picked(nrm[t], rec_t, slice(lo, hi)), ACT.Copy)
 
-        def fetch_prev(t, c):
-            lo, hi = CHUNKS[c]
-            nc.scalar.activation(prev[c][:, t, :], nrm[t][:].indirect(rec_t[:, lo // 16 : hi // 16]), ACT.Copy)
+        def own_on_vector(t, a):
+            nc.vector.scalar_tensor_tensor(own[:, t, HALVES[a]], y[t][a], -1.25, nrm[t][:, HALVES[a]], ALU.mult, ALU.mult)
 
-        BANKS = ["y0_0", "y0_1", "y1", "y2", "y3"]
-        stay_v(0)
-        stay_v(1)
-        stay_v(2)
-        stay_v(3)
+        def y_to_sbuf(t, parts, tag):
+            y_sb = floats("y_sb%d" % t, parts[-1][0].stop, tag=tag)
+            for cols, part in parts:
+                nc.scalar.activation(y_sb[:, cols], part, ACT.Copy, scale=-1.25)
+            return y_sb
+
+        def own_on_gpsimd(t, cols, y_sb):
+            nc.gpsimd.tensor_tensor(own[:, t, cols], y_sb[:], nrm[t][:, cols], ALU.mult)
+
+        nc.vector.tensor_copy(w_bf[:].rearrange("p (c i) r -> p c r i", i=4), w_raw[:].rearrange("p r (c i) -> p c r i", i=4))
+        nc.vector.quantize_mx(out=w_codes[:].bitcast(FP8X4), scales=w_scales[:], in_=w_bf[:].rearrange("p n r -> p (n r)"))
+        stay_on_vector(0)
+        stay_on_vector(1)
+
         emission(0)
-        fetch_er(0, 512)
+        for cols in HALVES:
+            nc.vector.tensor_copy(er[0][:, cols], picked(em_win[0], rec_t, cols))
         emission(1)
-        fetch_er(1, 0)
-        nc.scalar.activation(gain[:], unit_t[:], ACT.Copy, scale=-0.8)
-        mixed_part(0, 0)
-        mixed_part(0, 1)
-        posterior_part(0, 0)
-        posterior_part(0, 1)
-        group_sum(0)
-        invert_halves(0)
-        mixed(1)
-        posterior(1)
-        group_sum_turned(1, True)
-        normalise(0)
+        fetch_er(1)
+        posterior_by_halves(0)
+        members = post[0].rearrange("p (v d) -> p v d", d=D)
+        pair_sums = sb.tile([P, GROUPS, 2], F32, name="pair_sums")
+        sums_0 = floats("sums_0", GROUPS)
+        inverse_0 = floats("inverse0", GROUPS)
+        nc.vector.tensor_tensor(pair_sums[:], members[:, :, 0:2], members[:, :, 2:4], ALU.add)
+        nc.vector.scalar_tensor_tensor(sums_0[:], pair_sums[:, :, 0], 0.2, pair_sums[:, :, 1], ALU.add, ALU.add)
+        mixed(1, WHOLE)
+        stay_on_vector(2)
+        posterior(1, WHOLE)
+        nc.vector.reciprocal(inverse_0[:], sums_0[:])
         emission(2)
-        fetch_er(2, 0)
-        emission(3)
-        fetch_er(3, 0)
-        own_term(0)
-        invert_halves(1)
-        turn_back(1)
-        mixed(2)
-        posterior(2)
-        group_sum_turned(2, True)
+        fetch_er(2)
+        nc.scalar.activation(gain[:], unit_t[:], ACT.Copy, scale=-0.8)
+        normalise(0, inverse_0)
+        emission(LAST)
+        fetch_er(LAST)
+        for cols in HALVES:
+            nc.scalar.activation(stay[LAST][:, cols], sw_raw[1][:, 1, cols], ACT.Copy, scale=-1.0, bias=1.0)
+        turned_1 = group_sums(1)
+        mixed(2, WHOLE)
+        posterior(2, WHOLE)
+        turned_2 = group_sums(2)
+        inverse_1 = invert(1, turned_1, "stay2")
+        posterior_by_halves(LAST)
+        turned_3 = group_sums(LAST)
 
-        normalise(1)
-        mixed(3)
-        posterior(3)
-        group_sum(3)
-        invert_halves(2)
-        turn_back(2)
-        invert_halves(3)
+        own_on_gpsimd(0, WHOLE, y_to_sbuf(0, list(zip(HALVES, y[0])), "er2"))
+        for cols in HALVES:
+            fetch_prev(0, cols.start, cols.stop)
+        y_sb_1 = y_to_sbuf(1, [(WHOLE, y[1][2])], "bent3")
+        normalise(1, turn_back(1, inverse_1))
+        own_on_gpsimd(1, WHOLE, y_sb_1)
+        inverse_2 = invert(2, turned_2, "er3")
+        inverse_3 = invert(LAST, turned_3, None)
+        y_sb_2 = y_to_sbuf(2, [(HALVES[0], y[2][1])], "em3")
+        back_2 = turn_back(2, inverse_2)
+        back_3 = turn_back(LAST, inverse_3)
+        normalise(2, back_2)
+        own_on_gpsimd(2, HALVES[1], y_sb_2)
+        normalise(LAST, back_3)
+        for cols in HALVES:
+            fetch_prev(1, cols.start, cols.stop)
+        for cols in HALVES:
+            fetch_prev(2, cols.start, cols.stop)
+            for lo in range(cols.start, cols.stop, P):
+                fetch_prev(LAST, lo, lo + P)
+        own_on_vector(2, 0)
+        own_on_vector(LAST, 0)
+        own_on_vector(LAST, 1)
 
-        for c in range(len(CHUNKS)):
-            fetch_prev(0, c)
-        round_w(nc.scalar.copy, "er3")
-        normalise(2)
-        normalise(3)
-        for c in range(len(CHUNKS)):
-            fetch_prev(1, c)
-        for c in range(len(CHUNKS)):
-            fetch_prev(2, c)
-        for c in range(len(CHUNKS)):
-            fetch_prev(3, c)
-        own_term(1)
-        own_term(2)
-        own_term(3)
-
+        free_banks = ["y0_0", "y0_1", "y1", "y2", "sum1", "sum2", "sum3"]
         out_rows = out.rearrange("(h p) j -> p h j", p=P)
-        for c, (lo, hi) in enumerate(CHUNKS):
-            cols = slice(lo, hi)
+        for c, (lo, hi) in enumerate(STRETCHES):
             width = hi - lo
             hid = sb.tile([P, width, PACK], BF16, name="hid%d" % c, align_bytes=64)
             nc.vector.tensor_tensor(
-                hid[:].rearrange("p (c i) t -> p c t i", i=4),
-                own[:, :, cols].rearrange("p t (c i) -> p c t i", i=4),
-                prev[c][:].rearrange("p t (c i) -> p c t i", i=4),
+                hid[:].rearrange("p (b i) t -> p b t i", i=2),
+                own[:, :, lo:hi].rearrange("p t (b i) -> p b t i", i=2),
+                prev[lo // HALF][:, :, lo % HALF : lo % HALF + width].rearrange("p t (b i) -> p b t i", i=2),
                 ALU.add)
             hid_codes = sb.tile([P, width], U32, name="hid_codes%d" % c, align_bytes=64)
             hid_scales = sb.tile([P, width], U8, name="hid_scales%d" % c, align_bytes=64)
             nc.vector.quantize_mx(out=hid_codes[:].bitcast(FP8X4), scales=hid_scales[:], in_=hid[:].rearrange("p j t -> p (j t)"))
-            last = c == len(CHUNKS) - 1
-            acc = [ps.tile([P, width], F32, name="acc_last%d" % h, tag=BANKS[c + h])[:] for h in range(2)] if last else None
-            if not last:
-                bank = ps.tile([P, 2, width], F32, name="acc%d" % c, tag=BANKS[c])
-                acc = [bank[:, h, :] for h in range(2)]
-            for h in range(N // P):
-                nc.tensor.matmul_mx(out=acc[h], lhsT=w_codes[:, h * P : (h + 1) * P].bitcast(FP8X4), lhsT_scale=w_scales[:, h * P : (h + 1) * P],
+            final = c == len(STRETCHES) - 1
+            if final:
+                acc = [ps.tile([P, width], F32, name="acc_final%d" % h, tag=free_banks[c + h])[:] for h in range(2)]
+            else:
+                both = ps.tile([P, 2, width], F32, name="acc%d" % c, tag=free_banks[c])
+                acc = [both[:, h, :] for h in range(2)]
+            for h in range(2):
+                dosages = slice(h * P, (h + 1) * P)
+                nc.tensor.matmul_mx(out=acc[h], lhsT=w_codes[:, dosages].bitcast(FP8X4), lhsT_scale=w_scales[:, dosages],
                                     rhs=hid_codes[:].bitcast(FP8X4), rhs_scale=hid_scales[:], start=True, stop=True)
             res = sb.tile([P, 2, width], F32, name="res%d" % c)
-            if last:
+            if final:
                 nc.scalar.copy(res[:, 0, :], acc[0])
                 nc.vector.tensor_copy(res[:, 1, :], acc[1])
             else:
-                nc.scalar.copy(res[:], bank[:])
-            nc.sync.dma_start(out_rows[:, :, cols], res[:])
+                nc.scalar.copy(res[:], both[:])
+            nc.sync.dma_start(out_rows[:, :, lo:hi], res[:])

from contextlib import ExitStack

import concourse.mybir as mybir
from concourse.masks import make_identity

K, S, T, D, N, H = 512, 512, 2048, 4, 256, 512
FLOPS = 2 * K * H * S + 2 * H * N * S

F32 = mybir.dt.float32
BF16 = mybir.dt.bfloat16
I32 = mybir.dt.int32
U32 = mybir.dt.uint32
U16 = mybir.dt.uint16
U8 = mybir.dt.uint8
FP8X4 = mybir.dt.float8_e4m3fn_x4
ALU = mybir.AluOpType
ACT = mybir.ActivationFunctionType

P = 128
PACK = 4
LANES = 16
GROUPS = S // D
HALF = S // 2
WHOLE = slice(0, S)
HALVES = (slice(0, HALF), slice(HALF, S))
LAST = PACK - 1
STRETCHES = ((0, 128), (128, 256), (256, 320), (320, 384), (384, 448), (448, 512))


def tile_picked_ypopgn_dos_p_kernel(tc, x_words, x_scales, hT, sw, unit, w1, offs, rec, out):
    nc = tc.nc
    with ExitStack() as ctx:
        sb = ctx.enter_context(tc.tile_pool(name="sb", bufs=1))
        ps = ctx.enter_context(tc.psum_pool(name="ps", bufs=1))

        def floats(name, width, tag=None):
            return sb.tile([P, width], F32, name=name, tag=tag or name, align_bytes=64)

        def row_tiles(name, width):
            return [floats("%s%d" % (name, t), width) for t in range(PACK)]

        def picked(window, places, cols):
            return window[:].indirect(places[:, cols.start // LANES : cols.stop // LANES])

        offs_t = sb.tile([P, S // LANES], U16, name="offs_t")
        rec_t = sb.tile([P, S // LANES], U16, name="rec_t")
        words = sb.tile([P, T], U32, name="words", align_bytes=64)
        scales = sb.tile([P, T], U8, name="scales", align_bytes=64)
        h_raw = sb.tile([P, PACK, H], F32, name="h_raw")
        sw_raw = [sb.tile([P, 2, S], F32, name="sw_raw%d" % a) for a in range(2)]
        w_raw = sb.tile([P, PACK, N], F32, name="w_raw")
        unit_t = sb.tile([P, PACK], F32, name="unit_t")

        nc.vector.memset(scales[:].bitcast(I32), 0)
        sw_rows = sw.rearrange("(p t) j -> p t j", t=PACK)
        nc.sync.dma_start(h_raw[:], hT.rearrange("(p r) c -> p r c", r=PACK))
        nc.sync.dma_start(offs_t[:], offs)
        for a in range(4):
            nc.sync.dma_start(scales[a:P:32, :].bitcast(I32), x_scales[0, a:16:4, :].bitcast(I32))
        nc.sync.dma_start(words[:].bitcast(I32), x_words[0].rearrange("p c r -> p (c r)").bitcast(I32))
        nc.sync.dma_start(w_raw[:], w1.rearrange("(p r) n -> p r n", r=PACK))
        nc.sync.dma_start(sw_raw[0][:], sw_rows[:, 0:2, :])
        nc.sync.dma_start(rec_t[:], rec)
        nc.sync.dma_start(sw_raw[1][:], sw_rows[:, 2:4, :])
        nc.sync.dma_start(unit_t[:], unit.rearrange("(p t) o -> p (t o)", t=PACK))
        ident = sb.tile([P, P], F32, name="ident")
        make_identity(nc, ident[:])

        scales_g = sb.tile([P, S], U8, name="scales_g", align_bytes=64)
        words_g = [sb.tile([P, HALF], U32, name="words_g%d" % a, align_bytes=64) for a in range(2)]
        h_bf = [sb.tile([P, 2, P, PACK], BF16, name="h_bf%d" % a, align_bytes=64) for a in range(2)]
        h_cols = h_raw[:].rearrange("p r (m t) -> p m r t", t=PACK)
        nc.vector.tensor_copy(h_bf[0][:].rearrange("p u m r -> p m r u"), h_cols[:, :, :, 0:2])
        nc.scalar.copy(h_bf[1][:].rearrange("p u m r -> p m r u"), h_cols[:, :, :, 2:4])
        nc.vector.tensor_copy(scales_g[:], picked(scales, offs_t, WHOLE))
        h_codes = sb.tile([P, H], U32, name="h_codes", tag="scales", align_bytes=64)
        h_scales = sb.tile([P, H], U8, name="h_scales", align_bytes=64)
        for a in range(2):
            pair = slice(a * 2 * P, (a + 1) * 2 * P)
            nc.vector.quantize_mx(out=h_codes[:, pair].bitcast(FP8X4), scales=h_scales[:, pair],
                                  in_=h_bf[a][:].rearrange("p u m r -> p (u m r)"))
        for a in range(2):
            nc.vector.tensor_copy(words_g[a][:], picked(words, offs_t, HALVES[a]))
        y = [[ps.tile([P, HALF], F32, name="y0_%d" % a)[:] for a in range(2)]]
        for t in range(1, PACK):
            bank = ps.tile([P, S], F32, name="y%d" % t)
            y.append([bank[:, cols] for cols in HALVES] + [bank[:]])
        for t in range(PACK):
            profiles = slice(t * P, (t + 1) * P)
            for a in range(2):
                nc.tensor.matmul_mx(out=y[t][a], lhsT=h_codes[:, profiles].bitcast(FP8X4), lhsT_scale=h_scales[:, profiles],
                                    rhs=words_g[a][:].bitcast(FP8X4), rhs_scale=scales_g[:, HALVES[a]], start=True, stop=True)

        stay, er, nrm = row_tiles("stay", S), row_tiles("er", S), row_tiles("nrm", S)
        em_win = row_tiles("em", S + 1)
        avg = row_tiles("avg", 1)
        mix = [floats("mix%d" % t, S, tag="mix") for t in range(PACK)]
        own = sb.tile([P, PACK, S], F32, name="own", tag="mix", align_bytes=64)
        prev = [sb.tile([P, PACK, HALF], F32, name="prev%d" % a) for a in range(2)]
        post = [floats("post%d" % t, S)[:] for t in range(LAST)] + [prev[1][:, 2:4, :].rearrange("p t j -> p (t j)")]
        gain = sb.tile([P, PACK], F32, name="gain")
        w_bf = sb.tile([P, N, PACK], BF16, name="w_bf", align_bytes=64)
        w_codes = sb.tile([P, N], U32, name="w_codes", align_bytes=64)
        w_scales = sb.tile([P, N], U8, name="w_scales", align_bytes=64)
        floor = sb.tile([P, P], F32, name="floor")
        nc.gpsimd.memset(floor[:], 1.0)
        nc.gpsimd.tensor_scalar(floor[:], floor[:], 0.2, 0.0, ALU.mult, ALU.add)

        def emission(t):
            bent = floats("bent%d" % t, S)
            for a in range(2):
                nc.scalar.activation(bent[:, HALVES[a]], y[t][a], ACT.Tanh)
            nc.scalar.activation(em_win[t][:, :S], bent[:], ACT.Exp, scale=1.1, accum_out=em_win[t][:, S:])
            nc.scalar.activation(avg[t][:], em_win[t][:, S:], ACT.Copy, scale=1.0 / S)

        def stay_on_vector(t):
            nc.vector.tensor_scalar(stay[t][:], sw_raw[t // 2][:, t % 2, :], -1.0, 1.0, ALU.mult, ALU.add)

        def fetch_er(t):
            nc.scalar.activation(er[t][:], picked(em_win[t], rec_t, WHOLE), ACT.Copy)

        def mixed(t, cols):
            nc.vector.scalar_tensor_tensor(mix[t][:, cols], er[t][:, cols], avg[t][:], stay[t][:, cols], ALU.subtract, ALU.mult)

        def posterior(t, cols):
            nc.vector.scalar_tensor_tensor(post[t][:, cols], mix[t][:, cols], avg[t][:], em_win[t][:, cols], ALU.add, ALU.mult)

        def posterior_by_halves(t):
            for step in (mixed, posterior):
                for cols in HALVES:
                    step(t, cols)

        def group_sums(t):
            turned = ps.tile([P, P], F32, name="turned%d" % t, tag="sum%d" % t)
            members = post[t].rearrange("p (v d) -> p v d", d=D)
            terms = [floor[:]] + [members[:, :, d] for d in range(D)]
            for n, term in enumerate(terms):
                nc.tensor.matmul(out=turned[:], lhsT=term, rhs=ident[:], is_transpose=True, start=n == 0, stop=n == D)
            return turned

        def invert(t, turned, tag):
            inverse = floats("inverse%d" % t, GROUPS, tag=tag)
            nc.vector.reciprocal(inverse[:], turned[:])
            return inverse

        def turn_back(t, inverse):
            back = ps.tile([P, GROUPS], F32, name="back%d" % t, tag="sum%d" % t)
            nc.tensor.transpose(back[:], inverse[:], ident[:])
            return back

        def normalise(t, inverse):
            nc.vector.scalar_tensor_tensor(
                nrm[t][:].rearrange("p (v d) -> p v d", d=D), post[t].rearrange("p (v d) -> p v d", d=D), gain[:, t : t + 1],
                inverse[:].unsqueeze(2).to_broadcast([P, GROUPS, D]), ALU.mult, ALU.mult)

        def fetch_prev(t, lo, hi):
            first = lo % HALF
            nc.scalar.activation(prev[lo // HALF][:, t, first : first + hi - lo], picked(nrm[t], rec_t, slice(lo, hi)), ACT.Copy)

        def own_on_vector(t, a):
            nc.vector.scalar_tensor_tensor(own[:, t, HALVES[a]], y[t][a], -1.25, nrm[t][:, HALVES[a]], ALU.mult, ALU.mult)

        def y_to_sbuf(t, parts, tag):
            y_sb = floats("y_sb%d" % t, parts[-1][0].stop, tag=tag)
            for cols, part in parts:
                nc.scalar.activation(y_sb[:, cols], part, ACT.Copy, scale=-1.25)
            return y_sb

        def own_on_gpsimd(t, cols, y_sb):
            nc.gpsimd.tensor_tensor(own[:, t, cols], y_sb[:], nrm[t][:, cols], ALU.mult)

        nc.vector.tensor_copy(w_bf[:].rearrange("p (c i) r -> p c r i", i=4), w_raw[:].rearrange("p r (c i) -> p c r i", i=4))
        nc.vector.quantize_mx(out=w_codes[:].bitcast(FP8X4), scales=w_scales[:], in_=w_bf[:].rearrange("p n r -> p (n r)"))
        stay_on_vector(0)
        stay_on_vector(1)

        emission(0)
        for cols in HALVES:
            nc.vector.tensor_copy(er[0][:, cols], picked(em_win[0], rec_t, cols))
        emission(1)
        fetch_er(1)
        posterior_by_halves(0)
        members = post[0].rearrange("p (v d) -> p v d", d=D)
        pair_sums = sb.tile([P, GROUPS, 2], F32, name="pair_sums")
        sums_0 = floats("sums_0", GROUPS)
        inverse_0 = floats("inverse0", GROUPS)
        nc.vector.tensor_tensor(pair_sums[:], members[:, :, 0:2], members[:, :, 2:4], ALU.add)
        nc.vector.scalar_tensor_tensor(sums_0[:], pair_sums[:, :, 0], 0.2, pair_sums[:, :, 1], ALU.add, ALU.add)
        mixed(1, WHOLE)
        stay_on_vector(2)
        posterior(1, WHOLE)
        nc.vector.reciprocal(inverse_0[:], sums_0[:])
        emission(2)
        fetch_er(2)
        nc.scalar.activation(gain[:], unit_t[:], ACT.Copy, scale=-0.8)
        normalise(0, inverse_0)
        emission(LAST)
        fetch_er(LAST)
        for cols in HALVES:
            nc.scalar.activation(stay[LAST][:, cols], sw_raw[1][:, 1, cols], ACT.Copy, scale=-1.0, bias=1.0)
        turned_1 = group_sums(1)
        mixed(2, WHOLE)
        posterior(2, WHOLE)
        turned_2 = group_sums(2)
        inverse_1 = invert(1, turned_1, "stay2")
        posterior_by_halves(LAST)
        turned_3 = group_sums(LAST)

        own_on_gpsimd(0, WHOLE, y_to_sbuf(0, list(zip(HALVES, y[0])), "er2"))
        for cols in HALVES:
            fetch_prev(0, cols.start, cols.stop)
        y_sb_1 = y_to_sbuf(1, [(WHOLE, y[1][2])], "bent3")
        normalise(1, turn_back(1, inverse_1))
        own_on_gpsimd(1, WHOLE, y_sb_1)
        inverse_2 = invert(2, turned_2, "er3")
        inverse_3 = invert(LAST, turned_3, None)
        y_sb_2 = y_to_sbuf(2, [(HALVES[0], y[2][1])], "em3")
        back_2 = turn_back(2, inverse_2)
        back_3 = turn_back(LAST, inverse_3)
        normalise(2, back_2)
        own_on_gpsimd(2, HALVES[1], y_sb_2)
        normalise(LAST, back_3)
        for cols in HALVES:
            fetch_prev(1, cols.start, cols.stop)
        for cols in HALVES:
            fetch_prev(2, cols.start, cols.stop)
            for lo in range(cols.start, cols.stop, P):
                fetch_prev(LAST, lo, lo + P)
        own_on_vector(2, 0)
        own_on_vector(LAST, 0)
        own_on_vector(LAST, 1)

        free_banks = ["y0_0", "y0_1", "y1", "y2", "sum1", "sum2", "sum3"]
        out_rows = out.rearrange("(h p) j -> p h j", p=P)
        for c, (lo, hi) in enumerate(STRETCHES):
            width = hi - lo
            hid = sb.tile([P, width, PACK], BF16, name="hid%d" % c, align_bytes=64)
            nc.vector.tensor_tensor(
                hid[:].rearrange("p (b i) t -> p b t i", i=2),
                own[:, :, lo:hi].rearrange("p t (b i) -> p b t i", i=2),
                prev[lo // HALF][:, :, lo % HALF : lo % HALF + width].rearrange("p t (b i) -> p b t i", i=2),
                ALU.add)
            hid_codes = sb.tile([P, width], U32, name="hid_codes%d" % c, align_bytes=64)
            hid_scales = sb.tile([P, width], U8, name="hid_scales%d" % c, align_bytes=64)
            nc.vector.quantize_mx(out=hid_codes[:].bitcast(FP8X4), scales=hid_scales[:], in_=hid[:].rearrange("p j t -> p (j t)"))
            final = c == len(STRETCHES) - 1
            if final:
                acc = [ps.tile([P, width], F32, name="acc_final%d" % h, tag=free_banks[c + h])[:] for h in range(2)]
            else:
                both = ps.tile([P, 2, width], F32, name="acc%d" % c, tag=free_banks[c])
                acc = [both[:, h, :] for h in range(2)]
            for h in range(2):
                dosages = slice(h * P, (h + 1) * P)
                nc.tensor.matmul_mx(out=acc[h], lhsT=w_codes[:, dosages].bitcast(FP8X4), lhsT_scale=w_scales[:, dosages],
                                    rhs=hid_codes[:].bitcast(FP8X4), rhs_scale=hid_scales[:], start=True, stop=True)
            res = sb.tile([P, 2, width], F32, name="res%d" % c)
            if final:
                nc.scalar.copy(res[:, 0, :], acc[0])
                nc.vector.tensor_copy(res[:, 1, :], acc[1])
            else:
                nc.scalar.copy(res[:], both[:])
            nc.sync.dma_start(out_rows[:, :, lo:hi], res[:])
